import numpy as np, ml_dtypes
CORES = [3,7,11,15,131,135,139,143]
N = 8
BF = ml_dtypes.bfloat16
def gentries(a):
    return np.ascontiguousarray(a.reshape(8, 16, -1).transpose(0, 2, 1)).reshape(8, -1)
def gtable(e):
    e = np.asarray(e); return np.ascontiguousarray(e.reshape(8, -1, 16).transpose(0, 2, 1)).reshape(128, -1).astype(np.int32)
W, LW, C, B, KEYS, Q, RO = 2048, 11, 128, 16, 4, 11, 3
def pick(T, c):
    L = np.ascontiguousarray(c.transpose(0, 1, 3, 2)).reshape(N * 8, 16 * C)
    return np.stack([np.take(a, l, axis=1) for a, l in zip(T.reshape(N * 8, 16, W), L)]).reshape(N, 8, 16, C, 16)
def ask(D, X, c, y, w):
    d = pick(D, c); same = (d & (KEYS - 1)) == (c & (KEYS - 1))[..., None]
    cp = np.maximum(c, np.max(np.where(same, d, 0), axis=4))
    x = pick(X, cp); z = (np.max(x, axis=4) + np.min(x, axis=4)) >> 1
    u = np.add.reduce(w * z, axis=2, keepdims=True) & 4095
    return cp, z, u, B * np.arange(C) + (u & (B - 1)), np.abs(z - y)
def put(T, pl, val):
    np.put_along_axis(T, pl, val, axis=3)
def far(X, cp, v):
    return np.add.reduce(np.abs(pick(X, cp) - v[..., None]), axis=2)
def eve(D, X, c, y, w):
    cp, z, u, pl, v = ask(D, X, c, y, w); X = X.copy(); put(X, pl, v)
    return np.sort(far(X, np.roll(cp, 1, axis=0), np.roll(v, 1, axis=0)), axis=-1)[..., Q - 1]
def level(rng, q):
    return np.take_along_axis(np.sort(q, axis=-1), rng.integers(C // 4, 3 * C // 4, (N, 8, 1)), 2)[..., 0]
def sums(rng, tot):
    a = (tot[:, None, :] + np.arange(16).reshape(16, 1)) >> 4; hi, lo = a[:, :8], a[:, 8:]
    e = np.floor(rng.random((N, 8, C)) * (np.minimum(255 - hi, lo) + 1)).astype(np.int64)
    return rng.permuted(np.concatenate([hi + e, lo - e], axis=1), axis=1)
def parts(rng):
    D = rng.integers(0, W, (N, 8, 16, W)); X = (rng.random((N, 8, 16, W)) * rng.integers(64, 257, (N, 8, 1, W))).astype(np.int64)
    c = rng.integers(0, W, (N, 8, 16, C)); y = rng.integers(0, 256, (N, 8, 16, C)); w = rng.integers(0, 16, (N, 8, 16, C)); m = rng.integers(0, 2048, (N, 8, 16, 1))
    return D, X, c, y, w, m
def pack(D, X, c, y, w, m, th):
    return {"rec": (W * X + D).reshape(N, 128, W).astype(np.int32), "req": np.stack([gtable(a.transpose(0, 2, 1).reshape(8, 16 * C)) for a in c]),
            "aim": y.reshape(N, 128, C).astype(np.float32).astype(BF), "wt": w.reshape(N, 128, C).astype(np.float32).astype(BF),
            "mul": m.reshape(N, 128, 1).astype(np.int32), "th": np.repeat(th, 16, axis=1).reshape(N, 128, 1).astype(np.int32)}
def setup_inputs(rng):
    D, X, c, y, w, m = parts(rng)
    return pack(D, X, c, y, w, m, level(rng, eve(D, X, c, y, w)))
def setup_inputs_ties(rng):
    D, X, c, y, w, m = parts(rng); h = C // 2
    put(D, c[..., h:], (c[..., h:] + KEYS) & (W - 1)); put(D, c[..., :h], c[..., :h])
    z = ask(D, X, c, y, w)[1]
    y = np.where(rng.random((N, 8, 1, C)) < 0.3, np.minimum(np.maximum(z + rng.integers(-1, 2, z.shape), 0), 255), y)
    th = level(rng, eve(D, X, c, y, w)) + ((np.arange(8) + np.arange(N)[:, None]) & 1)
    return pack(D, X, c, y, w, m, th)
def setup_inputs_alike(rng):
    D, X, c, y, w, m = parts(rng)
    D[:, 1::2] += KEYS // 2 - (D[:, 1::2] & (KEYS - 1)); c[:, 1::2] += KEYS // 2 - (c[:, 1::2] & (KEYS - 1))
    c[:, 0] = rng.choice(np.array([0, W - 1, W // 2, 5]), (N, 16, C)); c[:, 4] = rng.choice(np.array([0, W - 1, W - 2, KEYS - 1, 7 * KEYS - 1]), (N, 16, C)); c[:, 6] = c[:, 6, :1]
    D[:, 2] = np.arange(W); D[:, 4] = W - 1; D[:, 6] = 0
    X[:, 4] = 255 * rng.integers(0, 2, (N, 1, W))
    return pack(D, X, c, y, w, m, level(rng, eve(D, X, c, y, w)))
def setup_inputs_ends(rng):
    D, X, c, y, w, m = parts(rng)
    th = rng.choice(np.array([0, 1, 4080, 4081]), (N, 8)); q = rng.permutation(N); th[q[0]] = 4081; th[q[1]] = 0
    w[:, 1] = 0
    X[:, 3, :2] = 255; X[:, 3, 2] = 15; w[:, 3] = 0; w[:, 3, 0] = 15; w[:, 3, 1:3] = 1; m[:, 3] = 2047
    y[:, 5] = 255 * rng.integers(0, 2, (N, 16, C)); w[:, 5] = 15; m[:, 5] = 0
    X[:, 7] = 255; y[:, 7] = 255; th[:, 7] = 4080 + (np.arange(N) & 1)
    return pack(D, X, c, y, w, m, th)
def setup_inputs_own(rng):
    D, X, c, y, w, m = parts(rng); lim = 4 * int(rng.integers(513, 1000)) + int(rng.integers(0, 2))
    X[:, :2, :, 1::2] = 255; c[:, :2] |= 1; w[:, :2] = w[:, :2, :1]
    y[:, 0] = sums(rng, rng.choice(np.array([0, 0, 1, 16]), (N, C))); y[:, 1] = sums(rng, lim + rng.integers(-2, 2, (N, C)))
    X[:, 2] = 255 - rng.integers(0, 17, (N, 16, W)); w[:, 2] = 14 + rng.integers(0, 2, (N, 16, C)); y[:, 2] = y[:, 2] * rng.integers(0, 2, (N, 1, C))
    for g, h in ((3, 127), (4, C - 1), (5, int(rng.choice(np.array([32, 63, 64, C // 2, C - 2]))))):
        D[:, g] = B * h; w[:, g] = 0; c[:, g] = KEYS * rng.integers(0, B * h // KEYS + 1, (N, 16, C))
        b = np.tile(rng.integers(0, 2, (1, 16)), (N, 1)); b[np.arange(N), rng.permutation(16)[:N]] ^= 1
        X[:, g, :, B * h] = KEYS * b; y[:, g] = KEYS * rng.integers(0, 2, (N, 16, C)); y[:, g, :, h] = KEYS
    c[:, 6, :, ::2] = 0; D[:, 6, :, 0] = 0; X[:, 6, :, 0] = 0; y[:, 6, :, 0] = 0
    D[:, 7] = np.arange(W); c[:, 7] = (B * (np.arange(C) + rng.integers(-1, 2, (N, 16, C))) + rng.integers(0, B, (N, 16, C))) & (W - 1)
    th = level(rng, eve(D, X, c, y, w))
    th[:, 0] = (np.arange(N) + int(rng.integers(0, 2))) & 1; th[:, 1] = lim; th[:, 3:6] = 8 * KEYS; th[:, 6] = rng.integers(1900, 2200, N)
    return pack(D, X, c, y, w, m, th)
def setup_inputs_spread(rng):
    D, X, c, y, w, m = parts(rng)
    def uneven(*shape):
        a = np.exp2(LW * rng.random(shape)).astype(np.int64) - 1
        return np.where(rng.random(shape[:-2] + (1, shape[-1])) < 0.5, a, W - 1 - a)
    D = np.where(rng.random((N, 8, 1, W)) < 0.5, uneven(N, 8, 16, W), D); c = np.where(rng.random((N, 8, 1, C)) < 0.5, uneven(N, 8, 16, C), c)
    X = (np.exp2(8 * rng.random((N, 8, 1, W))) * rng.random((N, 8, 16, W))).astype(np.int64)
    y = (np.exp2(8 * rng.random((N, 8, 1, C))) * rng.random((N, 8, 16, C))).astype(np.int64); w = w * (rng.random(w.shape) < rng.random((N, 8, 1, C)))
    m = (np.exp2(11 * rng.random(m.shape))).astype(np.int64)
    return pack(D, X, c, y, w, np.minimum(m, 2047), level(rng, eve(D, X, c, y, w)))
def check_inputs(d):
    bad = []
    for k, lo, hi in (("rec", 0, 256 * W - 1), ("req", 0, W - 1), ("aim", 0, 255), ("wt", 0, 15), ("mul", 0, 2047), ("th", 0, 4081)):
        a = np.asarray(d[k]).astype(np.float64)
        if not (np.min(a) >= lo and np.max(a) <= hi): bad.append("range of " + k)
        if not np.all(a == np.floor(a)): bad.append("whole numbers in " + k)
    a = np.asarray(d["th"]).reshape(N, 8, 16)
    if np.any(a != a[:, :, :1]): bad.append("th alike in the rows of a group")
    return bad
def reference(rec, req, aim, wt, mul, th):
    R = rec.astype(np.int64).reshape(N, 8, 16, W); D = R & (W - 1); X = R >> LW
    c = req.astype(np.int64).reshape(N, 8, 16, C)
    y = aim.astype(np.int64).reshape(N, 8, 16, C); w = wt.astype(np.int64).reshape(N, 8, 16, C)
    m = mul.astype(np.int64).reshape(N, 8, 16, 1); lim = th.astype(np.int64).reshape(N, 8, 16)[:, :, 0]
    odd = 2 * np.arange(16).reshape(16, 1) + 1
    for t in range(RO):
        cp, z, u, pl, v = ask(D, X, c, y, w)
        put(D, pl, cp); put(X, pl, v)
        sh = 1 + t % (N - 1)
        ca = np.roll(cp, sh, axis=0); va = np.roll(v, sh, axis=0); pa = np.roll(pl, sh, axis=0)
        near = np.add.reduce((far(X, ca, va) < lim[:, :, None, None]).astype(np.int64), axis=3)
        ok = (near >= Q)[:, :, None, :]
        put(D, pa, np.where(ok, ca, np.take_along_axis(D, pa, 3))); put(X, pa, np.where(ok, va, np.take_along_axis(X, pa, 3)))
        c = (((u * u) >> 5) + m * u + odd * z) & (W - 1)
    return {"yc": c.reshape(N, 128, C).astype(np.float32), "yz": z.reshape(N, 128, C).astype(np.float32).astype(BF), "yx": X.reshape(N, 128, W).astype(np.float32).astype(BF)}

from concourse.mybir import AluOpType, ActivationFunctionType as AF

STEPS = 3
MID = 7168
BIG = 131072.0
QUO = 10.5


def _sb(w, d):
    return ("sbuf", [128, w], d)


def _ps(w):
    return ("psum", [128, w], "float32")


SCRATCH = {
    "rec0": _sb(2048, "int32"), "dI": _sb(2048, "int32"), "dM": _sb(2048, "int32"), "etab": _sb(4096, "int32"),
    "xtab": _sb(4096, "int32"), "yxb": _sb(4096, "bfloat16"), "y": _sb(128, "bfloat16"), "w": _sb(128, "bfloat16"),
    "mI": _sb(8, "int32"), "thI": _sb(8, "int32"), "kcol": _sb(8, "float32"), "thf": _sb(8, "float32"), "odd": _sb(8, "float32"),
    "ones": _sb(2048, "float16"), "onesb": _sb(128, "bfloat16"), "onesf": _sb(128, "float32"), "expd": _sb(2048, "float16"),
    "sel": _sb(2048, "bfloat16"), "eyeh": _sb(128, "float16"), "eyeb": _sb(128, "bfloat16"), "neyeb": _sb(128, "bfloat16"),
    "bka": _sb(128, "float32"), "blkf": _sb(128, "float32"), "bkb": _sb(128, "bfloat16"), "blkb": _sb(128, "bfloat16"),
    "dgi": _sb(128, "int32"), "dgj": _sb(128, "int32"), "diag": _sb(128, "bfloat16"), "bsi": _sb(8, "int32"), "bsj": _sb(8, "int32"),
    "bsk": _sb(8, "int32"), "base": _sb(8, "int32"), "odi": _sb(8, "int32"), "odj": _sb(8, "int32"),
    "rmin": _sb(512, "float16"), "rmax": _sb(512, "float16"), "rz": _sb(128, "float32"),
    "cN": _sb(128, "int32"), "kc": _sb(128, "int32"), "m4": _sb(128, "int32"), "lst": _sb(128, "uint16"),
    "T4n": _sb(128, "float16"), "T4T": _sb(128, "float16"),
    "dg": _sb(2048, "float16"), "ya": _sb(2048, "float16"), "sc": _sb(2048, "float16"), "xh": _sb(2048, "float16"),
    "mx": _sb(2048, "float16"), "mn": _sb(2048, "float16"), "xa": _sb(2048, "bfloat16"), "dd": _sb(2048, "bfloat16"), "ad": _sb(2048, "bfloat16"),
    "t4": _sb(128, "float16"), "zi": _sb(128, "int32"), "wz": _sb(128, "float32"), "dv": _sb(128, "bfloat16"), "du": _sb(128, "int32"),
    "a15": _sb(8, "int32"), "pl": _sb(8, "uint16"), "uI": _sb(128, "int32"), "um": _sb(128, "int32"), "sq": _sb(128, "float32"),
    "q5": _sb(128, "int32"), "oz": _sb(128, "float32"), "r2": _sb(128, "int32"), "bb": _sb(128, "bfloat16"), "st": _sb(128, "float32"),
    "pb": _sb(8, "float32"), "nb": _sb(8, "float32"), "of": _sb(8, "uint16"), "ycb": _sb(128, "float32"), "yzb": _sb(128, "bfloat16"),
    "y0": _ps(512), "y1": _ps(512), "y2": _ps(512), "y3": _ps(512),
    "pT": _ps(512),
    "pU": _ps(256),
    "pV": _ps(512),
    "pD": _ps(128),
}
for _t in range(STEPS):
    SCRATCH["cl%d" % _t] = _sb(256, "uint16")
    SCRATCH["la%d" % _t] = _sb(256, "uint16")
    SCRATCH["vb%d" % _t] = _sb(136, "bfloat16")
    SCRATCH["lv%d" % _t] = _sb(136, "bfloat16")
PSUM = [k for k in SCRATCH if SCRATCH[k][0] == "psum"]
SEMAPHORES = ["qv", "qs", "qp", "qg", "loc"] + ["ld%d" % k for k in range(9)] + ["out%d" % k for k in range(3)] + \
    ["ac%d" % k for k in range(STEPS)] + ["av%d" % k for k in range(STEPS)]

D_V, D_S = ((0, 32), (32, 64), (64, 80)), ((96, 128), (80, 96))
BANKS = (0, 1, 3, 2)
X_V = ()
A_V = (112,)
X_SHIFT = (0, 1)
PE_J = (14, 15)
ABS_V = (4, 4, 3, 2, 1)


def R(name, lo, hi, st=1):
    return (name, lo, hi, st)


def I(win, off):
    return ("indirect", win, off)


def rank_program(g, core, T, topo):
    rank = T.rank_of(core)
    if rank is None:
        return
    A = AluOpType
    N = len(T.cores)
    queues = {"v": g.vector, "s": g.scalar, "p": g.tensor, "g": g, "y": g.sync}
    count = {q: 0 for q in "vspg"}
    seen = {q: {} for q in queues}
    clock = {}
    last_w, last_r = {}, {}
    target = {}
    for q in "vspg":
        target[q] = (lambda s: lambda n: (s, n))(T.sem["q" + q])

    def flat(x):
        return [x[1], x[2]] if x[0] == "indirect" else [x]

    def ap(x):
        if x[0] == "indirect":
            return ap(x[1]).indirect(ap(x[2]))
        return T[x[0]][:, x[1]:x[2]] if x[3] == 1 else T[x[0]][:, x[1]:x[2]:x[3]]

    def need(q, reads, writes):
        want = {}

        def add(src, n):
            want[src] = max(want.get(src, 0), n)
        for (b, lo, hi, _s), wr in [(r, False) for r in reads] + [(w, True) for w in writes]:
            ps = b in PSUM
            for (l, h, src, n) in last_w.get(b, []):
                if (ps or (l < hi and lo < h)) and not (ps and q == "p" and src == "p"):
                    add(src, n)
            for (l, h, src, n) in last_r.get(b, []):
                if src != q and (ps or (wr and l < hi and lo < h)):
                    add(src, n)
        while want:
            src = max(want, key=lambda s: (s in "vspg", want[s]))
            n = want.pop(src)
            if seen[q].get(src, 0) >= n:
                continue
            sem, val = target[src](n)
            queues[q].wait_ge(sem, val)
            seen[q][src] = n
            for k, m in clock.get((src, n), {}).items():
                if seen[q].get(k, 0) < m:
                    seen[q][k] = m

    def record(src, n, reads, writes):
        for (b, lo, hi, _s) in writes:
            keep = [e for e in last_w.get(b, []) if not (lo <= e[0] and e[1] <= hi and (e[2] == src or b not in PSUM))]
            last_w[b] = keep + [(lo, hi, src, n)]
            if b not in PSUM:
                last_r[b] = [e for e in last_r.get(b, []) if not (lo <= e[0] and e[1] <= hi)]
        for (b, lo, hi, _s) in reads:
            keep = [e for e in last_r.get(b, []) if not (lo <= e[0] and e[1] <= hi and e[2] == src)]
            last_r[b] = keep + [(lo, hi, src, n)]

    def op(q, call, outs, ins):
        reads = [r for x in ins for r in flat(x)]
        writes = []
        for x in outs:
            writes.append(flat(x)[0])
            reads += flat(x)[1:]
        need(q, reads, writes)
        i = call()
        count[q] += 1
        i.then_inc(T.sem["q" + q], 1)
        clock[(q, count[q])] = dict(seen[q])
        record(q, count[q], reads, writes)

    def event(name, sem, val, writes):
        target[name] = lambda n: (sem, val)
        record(name, 1, [], writes)

    def cp(o, i):
        op("v", lambda: g.vector.tensor_copy(ap(o), ap(i)), [o], [i])

    def tt(o, a, b, f):
        op("v", lambda: g.vector.tensor_tensor(ap(o), ap(a), ap(b), f), [o], [a, b])

    def ts(o, a, s1, f1, s2=None, f2=None):
        col = isinstance(s1, tuple)
        k1 = ap(s1) if col else s1
        more = () if f2 is None else (f2,)
        op("v", lambda: g.vector.tensor_scalar(ap(o), ap(a), k1, s2, f1, *more), [o], [a, s1] if col else [a])

    def scan(o, a, b, f0, f1):
        op("v", lambda: g.vector.tensor_tensor_scan(ap(o), ap(a), ap(b), 0.0, f0, f1), [o], [a, b])

    def fill(o, c):
        op("v", lambda: g.vector.memset(ap(o), c), [o], [])

    def act(o, i, f=AF.Identity, bias=0.0, scale=1.0):
        col = isinstance(scale, tuple)
        k = ap(scale) if col else scale
        op("s", lambda: g.scalar.activation(ap(o), ap(i), f, bias=bias, scale=k), [o], [i, scale] if col else [i])

    def mm(o, l, r, start, stop):
        op("p", lambda: g.tensor.matmul(ap(o), ap(l), ap(r), start, stop), [o], [l, r])

    def asel(o, i, pat, f, base, cm):
        op("g", lambda: g.affine_select(ap(o), ap(i), pat, f, 0.0, base, cm), [o], [i])

    def iota(o, pat, base, cm):
        op("g", lambda: g.iota(ap(o), pat, base, cm), [o], [])

    nload = [0]

    def load(q, out, src):
        sem = T.sem["ld%d" % nload[0]]
        queues[q].dma_start(ap(out), src).then_inc(sem, 16)
        event("ld%d" % nload[0], sem, 16, [out])
        nload[0] += 1
    C = (0, 128)
    blocks = [(512 * b, 512 * b + 512) for b in range(4)]
    load("y", R("cN", *C), T.req[:])
    for b, k in enumerate(blocks):
        load("y" if b & 1 else "s", R("rec0", *k), T.rec[:, k[0]:k[1]])
    load("y", R("w", *C), T.wt[:])
    load("y", R("y", *C), T.aim[:])
    load("y", R("mI", 0, 1), T.mul[:])
    load("y", R("thI", 0, 1), T.th[:])

    fill(R("ones", 0, 2048), 1.0)
    fill(R("onesb", *C), 1.0)
    fill(R("onesf", *C), 1.0)
    asel(R("eyeh", *C), R("ones", *C), [[-1, 128]], A.is_equal, 0, 1)
    asel(R("expd", 0, 2048), R("ones", 0, 2048), [[-1, 128], [0, 16]], A.is_equal, 0, 1)
    iota(R("dgi", *C), [[-1, 128]], 256, 1)
    asel(R("eyeb", *C), R("onesb", *C), [[-1, 128]], A.is_equal, 0, 1)
    asel(R("bka", *C), R("onesf", *C), [[-16, 8], [0, 16]], A.is_ge, 0, 1)
    asel(R("blkf", *C), R("bka", *C), [[16, 8], [0, 16]], A.is_ge, 15, -1)
    iota(R("bsi", 0, 8), [[0, 8]], 0, 16)
    iota(R("bsk", 0, 8), [[256, 8]], 0, 0)
    iota(R("odi", 0, 8), [[0, 8]], 0, 1)
    asel(R("bkb", *C), R("onesb", *C), [[-16, 8], [0, 16]], A.is_ge, 0, 1)
    asel(R("blkb", *C), R("bkb", *C), [[16, 8], [0, 16]], A.is_ge, 15, -1)
    op("g", lambda: g.iota(ap(R("sel", 0, 2048)), [[0, 2048]], 0, 0, allow_small_or_imprecise_dtypes=True), [R("sel", 0, 2048)], [])

    ts(R("kc", *C), R("cN", *C), 3, A.bitwise_and)
    act(R("T4n", *C), R("kc", *C), scale=-4096.0, bias=float(MID - 2044))
    cp(R("lst", *C), R("cN", *C))
    for b, k in enumerate(blocks):
        ts(R("dI", *k), R("rec0", *k), 2047, A.bitwise_and)
        act(R("dM", *k), R("dI", *k), scale=4097.0)
        if b:
            ts(R("etab", *blocks[b - 1]), R("dM", *blocks[b - 1]), 14332, A.bitwise_and)
    mm(R("pT", *C), R("T4n", *C), R("eyeh", *C), True, True)
    ts(R("etab", *blocks[3]), R("dM", *blocks[3]), 14332, A.bitwise_and)

    def bounds():
        act(R("T4T", *C), R("pT", *C))
        for b in BANKS:
            mm(R("y%d" % b, 0, 512), R("T4T", *C), R("expd", 512 * b, 512 * b + 512), True, False)

    def own():
        act(R("pT", 384, 512), R("m4", *C), scale=-1.0, bias=2044.0)
        act(R("pT", 128, 256), R("kc", *C), bias=2044.0)
        act(R("pT", 256, 384), R("kc", *C), scale=4096.0, bias=2044.0)

    ts(R("m4", *C), R("cN", *C), 2044, A.bitwise_and)
    bounds()
    own()

    sent = [0]

    def send(t, src, land, sem):
        dst = T.cores[(rank + 1 + t % (N - 1)) % N]
        back = T.cores[(rank - 1 - t % (N - 1)) % N]
        rid, pid = topo.addr(dst, core)
        eng = topo.engines(core, dst)[:8]
        n = len(topo.engines(back, core)[:8])
        width = SCRATCH[src][1][1]
        need("g", [R(src, 0, width)], [])
        g.remote_dma(T[land][:], T[src][:], T.sem[sem], T.sem.loc, pid, rid, sum(1 << e for e in eng))
        sent[0] += len(eng)
        event(sem, T.sem[sem], n, [R(land, 0, width)])

    E, X = R("etab", 0, 2048), R("xtab", 0, 2048)
    EW, XW, YW = R("etab", 0, 4096), R("xtab", 0, 4096), R("yxb", 0, 4096)
    pend = []
    for t in range(STEPS):
        last = t == STEPS - 1
        cl, la, vb, lv = "cl%d" % t, "la%d" % t, "vb%d" % t, "lv%d" % t
        for lo, hi in D_V:
            ts(R("dg", 16 * lo, 16 * hi), I(E, R("lst", lo, hi)), -float(MID), A.add)
        for lo, hi in D_S:
            act(R("dg", 16 * lo, 16 * hi), I(E, R("lst", lo, hi)), bias=-float(MID))
        for f in pend:
            f()
        pend = []
        if t == 0:
            fill(R("rmin", 0, 512), 0.0)
            fill(R("rmin", 0, 512, 16), 32768.0)
        for b in BANKS:
            k = (512 * b, 512 * b + 512)
            parts = sorted(r for r in D_V + D_S if 32 * b <= r[0] < 32 * b + 32)
            for n, (lo, hi) in enumerate(parts):
                mm(R("y%d" % b, 16 * lo - k[0], 16 * hi - k[0]), R("eyeh", *C), R("dg", 16 * lo, 16 * hi), False, n == len(parts) - 1)
            act(R("ya", *k), R("y%d" % b, 0, 512), AF.Abs)
        if t == 0:
            for b in range(4):
                if b in X_SHIFT:
                    ts(R("xtab", *blocks[b]), R("rec0", *blocks[b]), 11, A.arith_shift_right)
                else:
                    act(R("xtab", *blocks[b]), R("rec0", *blocks[b]), scale=2.0 ** -11, bias=-1023.5 / 2048)
            fill(R("rmax", 0, 512), 1.0)
            fill(R("rmax", 0, 512, 16), 0.0)
        for n, b in enumerate(BANKS):
            k = (512 * b, 512 * b + 512)
            scan(R("sc", *k), R("rmin", 0, 512), R("ya", *k), A.max, A.min)
            if n & 1:
                h = n // 2
                c = (64 * h, 64 * h + 64)
                tt(R("t4", *c), R("sc", 1024 * h + 15, 1024 * h + 1024, 16), R("pT", 384 + c[0], 384 + c[1]), A.min)
                tt(R(cl, *c), R("pT", 128 + c[0], 128 + c[1]), R("t4", *c), A.subtract)
        for lo in range(0, 128, 16):
            k, l = (16 * lo, 16 * lo + 256), R(cl, lo, lo + 16)
            if lo in X_V:
                ts(R("xh", *k), I(X, l), 0.5, A.mult, -0.125, A.add)
            else:
                act(R("xh", *k), I(X, l), bias=-0.125, scale=0.5)
        tt(R(cl, 128, 256), R("pT", 256, 384), R("t4", *C), A.subtract)
        send(t, cl, la, "ac%d" % t)
        if t == 0:
            ts(R("dgj", *C), R("dgi", *C), 15, A.bitwise_and)
            ts(R("diag", *C), R("dgj", *C), 0.0, A.is_equal, BIG, A.mult)
            cp(R("pV", 128, 256), R("w", *C))
            cp(R("pV", 256, 384), R("y", *C))
        for h in range(2):
            c = (64 * h, 64 * h + 64)
            mm(R("pU", *c), R("eyeb", *C), R("diag", *c), True, False)
            for b in (2 * h, 2 * h + 1):
                k = (512 * b, 512 * b + 512)
                scan(R("mx", *k), R("rmax", 0, 512), R("xh", *k), A.mult, A.max)
                scan(R("mn", *k), R("rmin", 0, 512), R("xh", *k), A.max, A.min)
            tt(R("zi", *c), R("mx", 1024 * h + 15, 1024 * h + 1024, 16), R("mn", 1024 * h + 15, 1024 * h + 1024, 16), A.add)
            tt(R("wz", *c), R("zi", *c), R("pV", 128 + c[0], 128 + c[1]), A.mult)
            mm(R("pU", *c), R("blkf", *C), R("wz", *c), False, True)
            tt(R("dv", *c), R("zi", *c), R("pV", 256 + c[0], 256 + c[1]), A.subtract)
        act(R(vb, *C), R("dv", *C), AF.Abs)
        if t == 0:
            fill(R("rz", *C), 1.0)
            fill(R("rz", 0, 128, 16), 0.0)
            ts(R("bsj", 0, 8), R("bsi", 0, 8), 255, A.bitwise_and)
            tt(R("base", 0, 8), R("bsj", 0, 8), R("bsk", 0, 8), A.add)
            ts(R("odj", 0, 8), R("odi", 0, 8), 15, A.bitwise_and)
            ts(R("odd", 0, 8), R("odj", 0, 8), 2.0, A.mult, 1.0, A.add)
            cp(R("kcol", 0, 1), R("mI", 0, 1))
            cp(R("thf", 0, 1), R("thI", 0, 1))
        act(R("oz", *C), R("zi", *C), scale=R("odd", 0, 1))
        scan(R("du", *C), R("rz", *C), R("pU", *C), A.mult, A.max)
        ts(R("a15", 0, 8), R("du", 15, 128, 16), 15, A.bitwise_and)
        tt(R("pl", 0, 8), R("a15", 0, 8), R("base", 0, 8), A.add)
        cp(R(vb, 128, 136), R("a15", 0, 8))
        send(t, vb, lv, "av%d" % t)
        cp(I(XW, R("pl", 0, 8)), R(vb, *C))
        act(R("uI", *C), R("pU", *C))
        if t == 0:
            act(R("neyeb", *C), R("eyeb", *C), scale=-1.0)
            for k in range(8):
                act(R("sel", 16 * k, 16 * k + 129 * 15 + 1, 129), R("blkb", 16 * k, 16 * k + 16))
        lo = 0
        while lo < 128:
            hi = lo + 16
            while lo not in A_V and hi < 128 and hi not in A_V and hi - lo < 64:
                hi += 16
            if lo not in A_V:
                act(R("xa", 16 * lo, 16 * hi), I(X, R(la, lo, hi)))
            lo = hi
        for lo in A_V:
            cp(R("xa", 16 * lo, 16 * lo + 256), I(X, R(la, lo, lo + 16)))
        for n, j in enumerate(PE_J):
            mm(R("y%d" % n, *C), R("eyeb", *C), R("xa", j, 2048, 16), True, False)
        ts(R("um", *C), R("uI", *C), 4095, A.bitwise_and)
        tt(R("sq", *C), R("um", *C), R("um", *C), A.mult)
        ts(R("q5", *C), R("sq", *C), -12.0, A.add, 2.0 ** -5, A.mult)
        ts(R("pV", 384, 512), R("um", *C), R("kcol", 0, 1), A.mult)
        tt(R("pV", 384, 512), R("oz", *C), R("pV", 384, 512), A.add)
        tt(R("r2", *C), R("q5", *C), R("pV", 384, 512), A.add)
        ts(R("cN", *C), R("r2", *C), 2047, A.bitwise_and)
        if last:
            for b in blocks:
                cp(R("yxb", *b), R("xtab", *b))
            cp(R("ycb", *C), R("cN", *C))
            cp(R("yzb", *C), R("zi", *C))
            for k, (o, b) in enumerate(((T.yc, "ycb"), (T.yz, "yzb"))):
                need("y", [R(b, *C)], [])
                g.sync.dma_start(o[:], T[b][:]).then_inc(T.sem["out%d" % k], 16)
        else:
            ts(R("kc", *C), R("cN", *C), 3, A.bitwise_and)
            act(R("T4n", *C), R("kc", *C), scale=-4096.0, bias=float(MID - 2044))
            mm(R("pT", *C), R("T4n", *C), R("eyeh", *C), True, True)
            act(R("T4T", *C), R("pT", *C))
            cp(R("lst", *C), R("cN", *C))
            ts(R("m4", *C), R("cN", *C), 2044, A.bitwise_and)
            cp(I(EW, R("pl", 0, 8)), R(cl, 128, 256))
        tt(R("pb", 0, 8), R(lv, 128, 136), R("base", 0, 8), A.add)
        mm(R("pV", *C), R("eyeb", *C), R(lv, *C), True, True)
        for n, j in enumerate(PE_J):
            mm(R("y%d" % n, *C), R("neyeb", *C), R(lv, *C), False, True)
        vj = [j for j in range(16) if j not in PE_J]
        for n, j in enumerate(vj):
            tt(R("dd", 128 * n, 128 * n + 128), R("xa", j, 2048, 16), R("pV", *C), A.subtract)
        todo = [(("y%d" % n, 0, 128, 1), [j]) for n, j in enumerate(PE_J)]
        n = 0
        for m in ABS_V:
            todo.append((R("dd", 128 * n, 128 * (n + m)), vj[n:n + m]))
            n += m
        n = 0
        for src, js in todo:
            act(R("ad", 128 * n, 128 * (n + len(js))), src, AF.Abs)
            for j in js:
                mm(R("pD", *C), R("sel", 128 * j, 128 * j + 128), R("ad", 128 * n, 128 * n + 128), n == 0, n == 15)
                n += 1
        mm(R("pU", 128, 256), R("eyeb", *C), R("diag", *C), True, False)
        ts(R("bb", *C), R("pD", *C), R("thf", 0, 1), A.is_lt)
        mm(R("pU", 128, 256), R("blkb", *C), R("bb", *C), False, True)
        if not last:
            for b in BANKS:
                mm(R("y%d" % b, 0, 512), R("T4T", *C), R("expd", 512 * b, 512 * b + 512), True, False)
            own()
        scan(R("st", *C), R("rz", *C), R("pU", 128, 256), A.mult, A.max)
        ts(R("nb", 0, 8), R("st", 15, 128, 16), BIG + QUO, A.is_lt, 2048.0, A.mult)
        tt(R("of", 0, 8), R("nb", 0, 8), R("pb", 0, 8), A.add)
        if last:
            cp(I(YW, R("of", 0, 8)), R(lv, *C))
        else:
            cp(I(EW, R("of", 0, 8)), R(la, 128, 256))
            pend.append((lambda l: lambda: cp(I(XW, R("of", 0, 8)), R(l, *C)))(lv))
    need("y", [R("yxb", 0, 2048)], [])
    g.sync.dma_start(T.yx[:], T.yxb[:, 0:2048]).then_inc(T.sem.out2, 16)
    g.wait_ge(T.sem.loc, sent[0])
    for k in range(3):
        g.sync.wait_ge(T.sem["out%d" % k], 16)
    for q in "vspg":
        if seen["y"].get(q, 0) < count[q]:
            g.sync.wait_ge(T.sem["q" + q], count[q])
